import numpy as np
import ml_dtypes


def mxq(x, axis, fmt="e4m3"):
    dtype, down = {"e4m3": (ml_dtypes.float8_e4m3fn, 7), "e5m2": (ml_dtypes.float8_e5m2, 14)}[fmt]
    v = np.moveaxis(np.asarray(x, np.float32).astype(ml_dtypes.bfloat16).astype(np.float64), axis, -1)
    blocks = v.reshape(v.shape[:-1] + (-1, 32))
    amax = np.abs(blocks).max(-1, keepdims=True)
    byte = np.maximum(np.where(amax > 0, np.frexp(amax)[1] - 1 + 127, 0) - down, 1)
    scale = np.exp2(byte - 127.0)
    codes = (blocks / scale).astype(np.float32).astype(dtype).astype(np.float64)
    return np.moveaxis((codes * scale).reshape(v.shape), -1, axis)


WIDE = False


def mx_kscale(k):
    if not WIDE:
        return np.ones(k)
    levels = np.array([10, -10, 5, -5, 0])
    if k % 512:
        return np.exp2(np.random.permutation(np.resize(levels, k // 32))).repeat(32)
    a = np.empty((k // 512, 16))
    for p in range(k // 512):
        a[p, :8] = np.random.permutation(np.resize(levels, 8))
        for g in range(8):
            far = levels[np.abs(levels - a[p, g]) >= 10]
            a[p, g + 8] = far[np.random.randint(len(far))]
    return np.exp2(a.ravel()).repeat(32)


def f64(x):
    return np.asarray(x).astype(np.float64)


def striped(idx):
    return np.tile(np.asarray(idx).reshape(-1, 16).T, (8, 1)).astype(np.uint16)


def unstriped(offs):
    return offs[:16].T.reshape(-1).astype(np.int64)


E2M1 = np.array([0.0, 0.5, 1.0, 1.5, 2.0, 3.0, 4.0, 6.0, -0.0, -0.5, -1.0, -1.5, -2.0, -3.0, -4.0, -6.0])


def pack_weight(w, fmt):
    k, n = w.shape
    w = f64(np.asarray(w, np.float32).astype(ml_dtypes.bfloat16)).reshape(k // 32, 32, n)
    amax = np.abs(w).max(1)
    if fmt == "e4m3":
        byte = np.frexp(amax)[1] - 1 + 127 - 7
    else:
        mant, ex = np.frexp(amax / 6.0)
        byte = np.where(mant > 0.5, ex, ex - 1) + 127
    byte = np.clip(np.where(amax > 0, byte, 1), 1, 254)
    scaled = (w * np.exp2(127.0 - byte)[:, None, :]).reshape(k, n).astype(np.float32)
    by_word = np.ascontiguousarray(scaled.reshape(k // 512, 128, 4, n).transpose(0, 1, 3, 2))
    if fmt == "e4m3":
        words = by_word.astype(ml_dtypes.float8_e4m3fn).view(np.uint8)
    else:
        c = by_word.astype(ml_dtypes.float4_e2m1fn).view(np.uint8) & 0xF
        words = (c[..., 0::2] | (c[..., 1::2] << 4)).reshape(k // 512, 128, 2 * n)
    return np.ascontiguousarray(words), np.ascontiguousarray(byte.astype(np.uint8).reshape(k // 512, 16, n))


def unpack_weight(words, scales, fmt):
    g, _, n = scales.shape
    words = np.ascontiguousarray(words).reshape(g, 128, n, -1)
    if fmt == "e4m3":
        vals = words.view(ml_dtypes.float8_e4m3fn).astype(np.float64)
    else:
        nib = np.empty((g, 128, n, 4), np.uint8)
        nib[..., 0::2] = words & 0xF
        nib[..., 1::2] = words >> 4
        vals = E2M1[nib]
    vals = vals * np.repeat(np.exp2(scales.astype(np.float64) - 127.0), 8, axis=1)[..., None]
    return vals.transpose(0, 1, 3, 2).reshape(g * 512, n)


K, T, J, R, O, N, E = 512, 1024, 256, 512, 128, 256, 256


def setup_inputs():
    n = np.random.standard_normal
    idx = np.random.permutation(T)[:J]
    idx2 = np.random.permutation(J)[:O]
    idx3 = np.random.permutation(E)[:O]
    fk = mx_kscale(K)
    fr = mx_kscale(R)
    xtp = pack_weight(n((K, T)) / fk[:, None], "e4m3")
    wp = pack_weight(n((K, R)) * 1 / np.sqrt(K) * fk[:, None], "e2m1")
    wbp = pack_weight(n((R, N)) * 1 / np.sqrt(R) / fr[:, None], "e4m3")
    return {
        "xt_words": xtp[0],
        "xt_scales": xtp[1],
        "w_words": wp[0],
        "w_scales": wp[1],
        "lo": (np.random.uniform(-1.0, 1.0, (R, 1)) + np.log(fr)[:, None]).astype(np.float32),
        "wb_words": wbp[0],
        "wb_scales": wbp[1],
        "so": (np.random.uniform(0.5, 1.6, (N, 1))).astype(np.float32),
        "offs": striped(idx),
        "offs2": striped(idx2),
        "offs3": striped(idx3),
    }


def reference(xt_words, xt_scales, w_words, w_scales, lo, wb_words, wb_scales, so, offs, offs2, offs3):
    idx = unstriped(offs)
    idx2 = unstriped(offs2)
    idx3 = unstriped(offs3)
    xtu = unpack_weight(xt_words, xt_scales, "e4m3")
    wu = unpack_weight(w_words, w_scales, "e2m1")
    wbu = unpack_weight(wb_words, wb_scales, "e4m3")
    xtidxg = xtu[:, idx]
    a = wu.T @ xtidxg
    nb = f64(lo) - np.max(a, axis=1, keepdims=True)
    hid = np.exp(a[:, idx2] + nb)
    hidq = mxq(hid, 0, "e4m3")
    p = wbu.T @ hidq
    y = np.zeros((N, E))
    y[:, idx3] = p * f64(so)
    return y

@@ -1,0 +1,137 @@
+from contextlib import ExitStack
+
+import concourse.mybir as mybir
+
+K, T, J, R, O, N, E = 512, 1024, 256, 512, 128, 256, 256
+FLOPS = 2 * K * R * J + 2 * R * N * O
+
+F32 = mybir.dt.float32
+BF16 = mybir.dt.bfloat16
+I32 = mybir.dt.int32
+U32 = mybir.dt.uint32
+U16 = mybir.dt.uint16
+U8 = mybir.dt.uint8
+FP8X4 = mybir.dt.float8_e4m3fn_x4
+FP4X4 = mybir.dt.float4_e2m1fn_x4
+ALU = mybir.AluOpType
+ACT = mybir.ActivationFunctionType
+
+P = 128
+PACK = 4
+QUADS = 4
+
+
+def tile_list_peaked_kernel(tc, xt_words, xt_scales, w_words, w_scales, lo, wb_words, wb_scales, so, offs, offs2, offs3, out):
+    nc = tc.nc
+    with ExitStack() as ctx:
+        lists = ctx.enter_context(tc.tile_pool(name="lists", bufs=1))
+        sb = ctx.enter_context(tc.tile_pool(name="sb", bufs=1))
+        psum = ctx.enter_context(tc.psum_pool(name="psum", bufs=1))
+
+        idx = lists.tile([P, J // 16], U16, name="idx")
+        idx2 = lists.tile([P, O // 16], U16, name="idx2")
+        idx3 = lists.tile([P, O // 16], U16, name="idx3")
+
+        x_words = sb.tile([P, T], I32, name="x_words", align_bytes=64)
+        x_plane = sb.tile([P, T // 4], I32, name="x_plane", align_bytes=64)
+        w_raw = sb.tile([P, R // 2], I32, name="w_raw", tag="weight", align_bytes=64)
+        ws_rows = sb.tile([4, QUADS, R // 4], I32, name="ws_rows", align_bytes=64)
+        ws_plane = sb.tile([P, R // 4], I32, name="ws_plane", align_bytes=64)
+        wb_plane = sb.tile([P, N // 4], I32, name="wb_plane", align_bytes=64)
+        lo_sb = sb.tile([P, PACK], F32, name="lo_sb")
+        so_sb = sb.tile([P, N // P], F32, name="so_sb")
+        pages = [sb.tile([P, E], F32, name="page%d" % h) for h in range(N // P)]
+
+        nc.vector.memset(x_plane[:], 0)
+        nc.vector.memset(ws_plane[:], 0)
+        for page in pages:
+            nc.gpsimd.memset(page[:], 0.0)
+        nc.gpsimd.memset(wb_plane[:], 0)
+
+        nc.sync.dma_start(idx[:], offs)
+        nc.scalar.dma_start(ws_rows[:], w_scales[0].bitcast(I32).rearrange("(q r) c -> r q c", r=4))
+        nc.sync.dma_start(x_words[:], xt_words[0].rearrange("p c t -> p (c t)").bitcast(I32))
+        xs32 = xt_scales[0].bitcast(I32)
+        for q in range(QUADS):
+            nc.scalar.dma_start(x_plane[32 * q : 32 * q + 4, :], xs32[4 * q : 4 * q + 4, :])
+        nc.sync.dma_start(w_raw[:], w_words[0].bitcast(I32))
+        nc.gpsimd.dma_start(lo_sb[:], lo.rearrange("(p t) o -> p (t o)", t=PACK))
+        nc.sync.dma_start(idx2[:], offs2)
+
+        for q in range(QUADS):
+            nc.vector.tensor_copy(ws_plane[32 * q : 32 * q + 4, :], ws_rows[:, q, :])
+        ws_dealt = sb.tile([P, R], U8, name="ws_dealt", align_bytes=64)
+        nc.vector.tensor_copy(
+            ws_dealt[:].rearrange("p (t m) -> p t m", t=PACK),
+            ws_plane[:].bitcast(U8).rearrange("p (m t) -> p t m", t=PACK),
+        )
+        w_dealt = []
+        for t in range(PACK):
+            dealt = sb.tile([P, 2 * P], U8, name="w_dealt%d" % t, align_bytes=64)
+            nc.scalar.copy(dealt[:].bitcast(U16), w_raw[:].bitcast(U16)[:, t : R : PACK])
+            w_dealt.append(dealt)
+
+        xg_plane = sb.tile([P, J], U8, name="xg_plane", align_bytes=64)
+        xg_words = sb.tile([P, J], U32, name="xg_words", align_bytes=64)
+        nc.vector.tensor_copy(xg_plane[:], x_plane[:].bitcast(U8).indirect(idx[:]))
+        nc.vector.tensor_copy(xg_words[:], x_words[:].bitcast(U32).indirect(idx[:]))
+
+        wb_sb = sb.tile([P, N], I32, name="wb_sb", tag="weight", align_bytes=64)
+        nc.sync.dma_start(wb_sb[:], wb_words[0].rearrange("p c t -> p (c t)").bitcast(I32))
+        wbs32 = wb_scales[0].bitcast(I32)
+        for q in range(QUADS):
+            nc.sync.dma_start(wb_plane[32 * q : 32 * q + 4, :], wbs32[4 * q : 4 * q + 4, :])
+        with nc.allow_non_contiguous_dma(reason="one value a partition and half"):
+            nc.sync.dma_start(so_sb[:], so.rearrange("(h p) o -> p (h o)", p=P))
+        nc.sync.dma_start(idx3[:], offs3)
+
+        HALF = O // 2
+        hid = [sb.tile([P, PACK * HALF], BF16, name="hid%d" % u, align_bytes=64) for u in range(2)]
+        a_sb = [sb.tile([P, J], F32, name="a_sb%d" % t) for t in range(PACK)]
+        nb = [sb.tile([P, 1], F32, name="nb%d" % t) for t in range(PACK)]
+
+        def look(t, u):
+            nc.scalar.activation(
+                hid[u][:, t : PACK * HALF : PACK], a_sb[t][:].indirect(idx2[:, 4 * u : 4 * u + 4]), ACT.Exp, bias=nb[t][:]
+            )
+
+        for t in range(PACK):
+            a_ps = psum.tile([P, J], F32, name="a_ps%d" % t)
+            nc.tensor.matmul_mx(
+                a_ps[:],
+                lhsT=w_dealt[t][:].bitcast(FP4X4),
+                lhsT_scale=ws_dealt[:, t * P : (t + 1) * P],
+                rhs=xg_words[:].bitcast(FP8X4),
+                rhs_scale=xg_plane[:],
+                start=True,
+                stop=True,
+            )
+            top = sb.tile([P, 1], F32, name="top%d" % t)
+            nc.vector.tensor_scalar(a_sb[t][:], a_ps[:], 1.0, None, ALU.mult, ALU.max, accum_out=top[:])
+            nc.gpsimd.tensor_scalar(nb[t][:], top[:], -1.0, lo_sb[:, t : t + 1], ALU.mult, ALU.add)
+            look(t, 0)
+        for t in range(PACK):
+            look(t, 1)
+
+        for u in range(2):
+            hid_codes = sb.tile([P, HALF], U32, name="hid_codes%d" % u, align_bytes=64)
+            hid_plane = sb.tile([P, HALF], U8, name="hid_plane%d" % u, align_bytes=64)
+            nc.vector.quantize_mx(hid_codes[:].bitcast(FP8X4), hid_plane[:], hid[u][:])
+            for h in range(N // P):
+                p_ps = psum.tile([P, HALF], F32, name="p_ps%d%d" % (u, h))
+                nc.tensor.matmul_mx(
+                    p_ps[:],
+                    lhsT=wb_sb[:, h * P : (h + 1) * P].bitcast(FP8X4),
+                    lhsT_scale=wb_plane[:].bitcast(U8)[:, h * P : (h + 1) * P],
+                    rhs=hid_codes[:].bitcast(FP8X4),
+                    rhs_scale=hid_plane[:],
+                    start=True,
+                    stop=True,
+                )
+                p_sb = sb.tile([P, HALF], F32, name="p_sb%d%d" % (u, h))
+                nc.vector.tensor_copy(p_sb[:], p_ps[:])
+                nc.scalar.activation(
+                    pages[h][:].indirect(idx3[:, 4 * u : 4 * u + 4]), p_sb[:], ACT.Copy, scale=so_sb[:, h : h + 1]
+                )
+        for h in range(N // P):
+            nc.sync.dma_start(out[h * P : (h + 1) * P, :], pages[h][:])

@@ -34,7 +34,7 @@ def tile_list_peaked_kernel(tc, xt_words, xt_scales, w_words, w_scales, lo, wb_w
 
         x_words = sb.tile([P, T], I32, name="x_words", align_bytes=64)
         x_plane = sb.tile([P, T // 4], I32, name="x_plane", align_bytes=64)
-        w_raw = sb.tile([P, R // 2], I32, name="w_raw", tag="weight", align_bytes=64)
+        w_raw = sb.tile([P, R // 2], I32, name="w_raw", align_bytes=64)
         ws_rows = sb.tile([4, QUADS, R // 4], I32, name="ws_rows", align_bytes=64)
         ws_plane = sb.tile([P, R // 4], I32, name="ws_plane", align_bytes=64)
         wb_plane = sb.tile([P, N // 4], I32, name="wb_plane", align_bytes=64)
@@ -45,26 +45,25 @@ def tile_list_peaked_kernel(tc, xt_words, xt_scales, w_words, w_scales, lo, wb_w
         nc.vector.memset(x_plane[:], 0)
         nc.vector.memset(ws_plane[:], 0)
         for page in pages:
-            nc.gpsimd.memset(page[:], 0.0)
-        nc.gpsimd.memset(wb_plane[:], 0)
+            nc.vector.memset(page[:], 0.0)
+        nc.vector.memset(wb_plane[:], 0)
 
         nc.sync.dma_start(idx[:], offs)
-        nc.scalar.dma_start(ws_rows[:], w_scales[0].bitcast(I32).rearrange("(q r) c -> r q c", r=4))
-        nc.sync.dma_start(x_words[:], xt_words[0].rearrange("p c t -> p (c t)").bitcast(I32))
+        nc.sync.dma_start(ws_rows[:], w_scales[0].bitcast(I32).rearrange("(q r) c -> r q c", r=4))
+        nc.sync.dma_start(w_raw[:], w_words[0].bitcast(I32))
         xs32 = xt_scales[0].bitcast(I32)
         for q in range(QUADS):
-            nc.scalar.dma_start(x_plane[32 * q : 32 * q + 4, :], xs32[4 * q : 4 * q + 4, :])
-        nc.sync.dma_start(w_raw[:], w_words[0].bitcast(I32))
-        nc.gpsimd.dma_start(lo_sb[:], lo.rearrange("(p t) o -> p (t o)", t=PACK))
+            queue = nc.sync if q < 2 else nc.scalar
+            queue.dma_start(x_plane[32 * q : 32 * q + 4, :], xs32[4 * q : 4 * q + 4, :])
+        nc.sync.dma_start(x_words[:], xt_words[0].rearrange("p c t -> p (c t)").bitcast(I32))
+        nc.sync.dma_start(lo_sb[:], lo.rearrange("(p t) o -> p (t o)", t=PACK))
         nc.sync.dma_start(idx2[:], offs2)
 
         for q in range(QUADS):
             nc.vector.tensor_copy(ws_plane[32 * q : 32 * q + 4, :], ws_rows[:, q, :])
-        ws_dealt = sb.tile([P, R], U8, name="ws_dealt", align_bytes=64)
-        nc.vector.tensor_copy(
-            ws_dealt[:].rearrange("p (t m) -> p t m", t=PACK),
-            ws_plane[:].bitcast(U8).rearrange("p (m t) -> p t m", t=PACK),
-        )
+        ws_by_t = ws_plane[:].bitcast(U8).rearrange("p (m t) -> p t m", t=PACK)
+        ws_dealt = [sb.tile([P, P], U8, name="ws_dealt%d" % t, align_bytes=64) for t in range(PACK)]
+        nc.vector.tensor_copy(ws_dealt[0][:], ws_by_t[:, 0, :])
         w_dealt = []
         for t in range(PACK):
             dealt = sb.tile([P, 2 * P], U8, name="w_dealt%d" % t, align_bytes=64)
@@ -75,12 +74,14 @@ def tile_list_peaked_kernel(tc, xt_words, xt_scales, w_words, w_scales, lo, wb_w
         xg_words = sb.tile([P, J], U32, name="xg_words", align_bytes=64)
         nc.vector.tensor_copy(xg_plane[:], x_plane[:].bitcast(U8).indirect(idx[:]))
         nc.vector.tensor_copy(xg_words[:], x_words[:].bitcast(U32).indirect(idx[:]))
+        for t in range(1, PACK):
+            nc.vector.tensor_copy(ws_dealt[t][:], ws_by_t[:, t, :])
 
-        wb_sb = sb.tile([P, N], I32, name="wb_sb", tag="weight", align_bytes=64)
-        nc.sync.dma_start(wb_sb[:], wb_words[0].rearrange("p c t -> p (c t)").bitcast(I32))
+        wb_sb = sb.tile([P, N], I32, name="wb_sb", align_bytes=64)
         wbs32 = wb_scales[0].bitcast(I32)
         for q in range(QUADS):
             nc.sync.dma_start(wb_plane[32 * q : 32 * q + 4, :], wbs32[4 * q : 4 * q + 4, :])
+        nc.sync.dma_start(wb_sb[:], wb_words[0].rearrange("p c t -> p (c t)").bitcast(I32))
         with nc.allow_non_contiguous_dma(reason="one value a partition and half"):
             nc.sync.dma_start(so_sb[:], so.rearrange("(h p) o -> p (h o)", p=P))
         nc.sync.dma_start(idx3[:], offs3)
@@ -100,7 +101,7 @@ def tile_list_peaked_kernel(tc, xt_words, xt_scales, w_words, w_scales, lo, wb_w
             nc.tensor.matmul_mx(
                 a_ps[:],
                 lhsT=w_dealt[t][:].bitcast(FP4X4),
-                lhsT_scale=ws_dealt[:, t * P : (t + 1) * P],
+                lhsT_scale=ws_dealt[t][:],
                 rhs=xg_words[:].bitcast(FP8X4),
                 rhs_scale=xg_plane[:],
                 start=True,
@@ -108,7 +109,7 @@ def tile_list_peaked_kernel(tc, xt_words, xt_scales, w_words, w_scales, lo, wb_w
             )
             top = sb.tile([P, 1], F32, name="top%d" % t)
             nc.vector.tensor_scalar(a_sb[t][:], a_ps[:], 1.0, None, ALU.mult, ALU.max, accum_out=top[:])
-            nc.gpsimd.tensor_scalar(nb[t][:], top[:], -1.0, lo_sb[:, t : t + 1], ALU.mult, ALU.add)
+            nc.scalar.activation(nb[t][:], top[:], ACT.Identity, bias=lo_sb[:, t : t + 1], scale=-1.0)
             look(t, 0)
         for t in range(PACK):
             look(t, 1)

@@ -19,28 +19,44 @@ ACT = mybir.ActivationFunctionType
 P = 128
 PACK = 4
 QUADS = 4
+QUAD = P // QUADS
+LIVE = 4
+WORD = 4
+GROUP = 16
+PAGES = N // P
+HALVES = 2
+HALF = O // HALVES
+HALF_COLS = HALF // GROUP
+MX_ALIGN = 64
 
 
 def tile_list_peaked_kernel(tc, xt_words, xt_scales, w_words, w_scales, lo, wb_words, wb_scales, so, offs, offs2, offs3, out):
     nc = tc.nc
+
+    def live_rows(plane, q):
+        return plane[QUAD * q : QUAD * q + LIVE, :]
+
+    def half_of(offsets, u):
+        return offsets[:, HALF_COLS * u : HALF_COLS * (u + 1)]
+
     with ExitStack() as ctx:
         lists = ctx.enter_context(tc.tile_pool(name="lists", bufs=1))
         sb = ctx.enter_context(tc.tile_pool(name="sb", bufs=1))
         psum = ctx.enter_context(tc.psum_pool(name="psum", bufs=1))
 
-        idx = lists.tile([P, J // 16], U16, name="idx")
-        idx2 = lists.tile([P, O // 16], U16, name="idx2")
-        idx3 = lists.tile([P, O // 16], U16, name="idx3")
+        idx = lists.tile([P, J // GROUP], U16, name="idx")
+        idx2 = lists.tile([P, O // GROUP], U16, name="idx2")
+        idx3 = lists.tile([P, O // GROUP], U16, name="idx3")
 
-        x_words = sb.tile([P, T], I32, name="x_words", align_bytes=64)
-        x_plane = sb.tile([P, T // 4], I32, name="x_plane", align_bytes=64)
-        w_raw = sb.tile([P, R // 2], I32, name="w_raw", align_bytes=64)
-        ws_rows = sb.tile([4, QUADS, R // 4], I32, name="ws_rows", align_bytes=64)
-        ws_plane = sb.tile([P, R // 4], I32, name="ws_plane", align_bytes=64)
-        wb_plane = sb.tile([P, N // 4], I32, name="wb_plane", align_bytes=64)
+        x_words = sb.tile([P, T], I32, name="x_words", align_bytes=MX_ALIGN)
+        x_plane = sb.tile([P, T // WORD], I32, name="x_plane", align_bytes=MX_ALIGN)
+        w_raw = sb.tile([P, 2 * R // WORD], I32, name="w_raw", align_bytes=MX_ALIGN)
+        ws_rows = sb.tile([LIVE, QUADS, R // WORD], I32, name="ws_rows", align_bytes=MX_ALIGN)
+        ws_plane = sb.tile([P, R // WORD], I32, name="ws_plane", align_bytes=MX_ALIGN)
+        wb_plane = sb.tile([P, N // WORD], I32, name="wb_plane", align_bytes=MX_ALIGN)
         lo_sb = sb.tile([P, PACK], F32, name="lo_sb")
-        so_sb = sb.tile([P, N // P], F32, name="so_sb")
-        pages = [sb.tile([P, E], F32, name="page%d" % h) for h in range(N // P)]
+        so_sb = sb.tile([P, PAGES], F32, name="so_sb")
+        pages = [sb.tile([P, E], F32, name="page%d" % h) for h in range(PAGES)]
 
         nc.vector.memset(x_plane[:], 0)
         nc.vector.memset(ws_plane[:], 0)
@@ -49,51 +65,50 @@ def tile_list_peaked_kernel(tc, xt_words, xt_scales, w_words, w_scales, lo, wb_w
         nc.vector.memset(wb_plane[:], 0)
 
         nc.sync.dma_start(idx[:], offs)
-        nc.sync.dma_start(ws_rows[:], w_scales[0].bitcast(I32).rearrange("(q r) c -> r q c", r=4))
-        nc.sync.dma_start(w_raw[:], w_words[0].bitcast(I32))
-        xs32 = xt_scales[0].bitcast(I32)
+        nc.scalar.dma_start(ws_rows[:], w_scales[0].bitcast(I32).rearrange("(q i) c -> i q c", i=LIVE))
+        nc.sync.dma_start(x_words[:], xt_words[0].rearrange("p c b -> p (c b)").bitcast(I32))
+        xs_rows = xt_scales[0].bitcast(I32)
         for q in range(QUADS):
-            queue = nc.sync if q < 2 else nc.scalar
-            queue.dma_start(x_plane[32 * q : 32 * q + 4, :], xs32[4 * q : 4 * q + 4, :])
-        nc.sync.dma_start(x_words[:], xt_words[0].rearrange("p c t -> p (c t)").bitcast(I32))
+            queue = nc.sync if q < QUADS // 2 else nc.scalar
+            queue.dma_start(live_rows(x_plane, q), xs_rows[LIVE * q : LIVE * (q + 1), :])
+        nc.sync.dma_start(w_raw[:], w_words[0].bitcast(I32))
         nc.sync.dma_start(lo_sb[:], lo.rearrange("(p t) o -> p (t o)", t=PACK))
         nc.sync.dma_start(idx2[:], offs2)
 
         for q in range(QUADS):
-            nc.vector.tensor_copy(ws_plane[32 * q : 32 * q + 4, :], ws_rows[:, q, :])
-        ws_by_t = ws_plane[:].bitcast(U8).rearrange("p (m t) -> p t m", t=PACK)
-        ws_dealt = [sb.tile([P, P], U8, name="ws_dealt%d" % t, align_bytes=64) for t in range(PACK)]
-        nc.vector.tensor_copy(ws_dealt[0][:], ws_by_t[:, 0, :])
+            nc.vector.tensor_copy(live_rows(ws_plane, q), ws_rows[:, q, :])
+        ws_by_set = ws_plane[:].bitcast(U8).rearrange("p (m t) -> p t m", t=PACK)
+        ws_dealt = [sb.tile([P, P], U8, name="ws_dealt%d" % t, align_bytes=MX_ALIGN) for t in range(PACK)]
+        nc.vector.tensor_copy(ws_dealt[0][:], ws_by_set[:, 0, :])
         w_dealt = []
         for t in range(PACK):
-            dealt = sb.tile([P, 2 * P], U8, name="w_dealt%d" % t, align_bytes=64)
-            nc.scalar.copy(dealt[:].bitcast(U16), w_raw[:].bitcast(U16)[:, t : R : PACK])
+            dealt = sb.tile([P, 2 * P], U8, name="w_dealt%d" % t, align_bytes=MX_ALIGN)
+            nc.scalar.copy(dealt[:].bitcast(U16), w_raw[:].bitcast(U16)[:, t:R:PACK])
             w_dealt.append(dealt)
 
-        xg_plane = sb.tile([P, J], U8, name="xg_plane", align_bytes=64)
-        xg_words = sb.tile([P, J], U32, name="xg_words", align_bytes=64)
-        nc.vector.tensor_copy(xg_plane[:], x_plane[:].bitcast(U8).indirect(idx[:]))
+        xg_plane = sb.tile([P, J], U8, name="xg_plane", align_bytes=MX_ALIGN)
+        xg_words = sb.tile([P, J], U32, name="xg_words", align_bytes=MX_ALIGN)
         nc.vector.tensor_copy(xg_words[:], x_words[:].bitcast(U32).indirect(idx[:]))
+        nc.vector.tensor_copy(xg_plane[:], x_plane[:].bitcast(U8).indirect(idx[:]))
         for t in range(1, PACK):
-            nc.vector.tensor_copy(ws_dealt[t][:], ws_by_t[:, t, :])
+            nc.vector.tensor_copy(ws_dealt[t][:], ws_by_set[:, t, :])
 
-        wb_sb = sb.tile([P, N], I32, name="wb_sb", align_bytes=64)
-        wbs32 = wb_scales[0].bitcast(I32)
+        wb_sb = sb.tile([P, N], I32, name="wb_sb", align_bytes=MX_ALIGN)
+        wbs_rows = wb_scales[0].bitcast(I32)
         for q in range(QUADS):
-            nc.sync.dma_start(wb_plane[32 * q : 32 * q + 4, :], wbs32[4 * q : 4 * q + 4, :])
-        nc.sync.dma_start(wb_sb[:], wb_words[0].rearrange("p c t -> p (c t)").bitcast(I32))
-        with nc.allow_non_contiguous_dma(reason="one value a partition and half"):
+            nc.sync.dma_start(live_rows(wb_plane, q), wbs_rows[LIVE * q : LIVE * (q + 1), :])
+        nc.sync.dma_start(wb_sb[:], wb_words[0].rearrange("p c b -> p (c b)").bitcast(I32))
+        with nc.allow_non_contiguous_dma(reason="so_sb[p, h] = so[128 h + p]: single values"):
             nc.sync.dma_start(so_sb[:], so.rearrange("(h p) o -> p (h o)", p=P))
         nc.sync.dma_start(idx3[:], offs3)
 
-        HALF = O // 2
-        hid = [sb.tile([P, PACK * HALF], BF16, name="hid%d" % u, align_bytes=64) for u in range(2)]
+        hid = [sb.tile([P, PACK * HALF], BF16, name="hid%d" % u, align_bytes=MX_ALIGN) for u in range(HALVES)]
         a_sb = [sb.tile([P, J], F32, name="a_sb%d" % t) for t in range(PACK)]
         nb = [sb.tile([P, 1], F32, name="nb%d" % t) for t in range(PACK)]
 
-        def look(t, u):
+        def fetch(t, u):
             nc.scalar.activation(
-                hid[u][:, t : PACK * HALF : PACK], a_sb[t][:].indirect(idx2[:, 4 * u : 4 * u + 4]), ACT.Exp, bias=nb[t][:]
+                hid[u][:, t : PACK * HALF : PACK], a_sb[t][:].indirect(half_of(idx2, u)), ACT.Exp, bias=nb[t][:]
             )
 
         for t in range(PACK):
@@ -110,15 +125,15 @@ def tile_list_peaked_kernel(tc, xt_words, xt_scales, w_words, w_scales, lo, wb_w
             top = sb.tile([P, 1], F32, name="top%d" % t)
             nc.vector.tensor_scalar(a_sb[t][:], a_ps[:], 1.0, None, ALU.mult, ALU.max, accum_out=top[:])
             nc.scalar.activation(nb[t][:], top[:], ACT.Identity, bias=lo_sb[:, t : t + 1], scale=-1.0)
-            look(t, 0)
+            fetch(t, 0)
         for t in range(PACK):
-            look(t, 1)
+            fetch(t, 1)
 
-        for u in range(2):
-            hid_codes = sb.tile([P, HALF], U32, name="hid_codes%d" % u, align_bytes=64)
-            hid_plane = sb.tile([P, HALF], U8, name="hid_plane%d" % u, align_bytes=64)
+        for u in range(HALVES):
+            hid_codes = sb.tile([P, HALF], U32, name="hid_codes%d" % u, align_bytes=MX_ALIGN)
+            hid_plane = sb.tile([P, HALF], U8, name="hid_plane%d" % u, align_bytes=MX_ALIGN)
             nc.vector.quantize_mx(hid_codes[:].bitcast(FP8X4), hid_plane[:], hid[u][:])
-            for h in range(N // P):
+            for h in range(PAGES):
                 p_ps = psum.tile([P, HALF], F32, name="p_ps%d%d" % (u, h))
                 nc.tensor.matmul_mx(
                     p_ps[:],
@@ -132,7 +147,7 @@ def tile_list_peaked_kernel(tc, xt_words, xt_scales, w_words, w_scales, lo, wb_w
                 p_sb = sb.tile([P, HALF], F32, name="p_sb%d%d" % (u, h))
                 nc.vector.tensor_copy(p_sb[:], p_ps[:])
                 nc.scalar.activation(
-                    pages[h][:].indirect(idx3[:, 4 * u : 4 * u + 4]), p_sb[:], ACT.Copy, scale=so_sb[:, h : h + 1]
+                    pages[h][:].indirect(half_of(idx3, u)), p_sb[:], ACT.Copy, scale=so_sb[:, h : h + 1]
                 )
-        for h in range(N // P):
+        for h in range(PAGES):
             nc.sync.dma_start(out[h * P : (h + 1) * P, :], pages[h][:])

from contextlib import ExitStack

import concourse.mybir as mybir

K, T, J, R, O, N, E = 512, 1024, 256, 512, 128, 256, 256
FLOPS = 2 * K * R * J + 2 * R * N * O

F32 = mybir.dt.float32
BF16 = mybir.dt.bfloat16
I32 = mybir.dt.int32
U32 = mybir.dt.uint32
U16 = mybir.dt.uint16
U8 = mybir.dt.uint8
FP8X4 = mybir.dt.float8_e4m3fn_x4
FP4X4 = mybir.dt.float4_e2m1fn_x4
ALU = mybir.AluOpType
ACT = mybir.ActivationFunctionType

P = 128
PACK = 4
QUADS = 4
QUAD = P // QUADS
LIVE = 4
WORD = 4
GROUP = 16
PAGES = N // P
HALVES = 2
HALF = O // HALVES
HALF_COLS = HALF // GROUP
MX_ALIGN = 64


def tile_list_peaked_kernel(tc, xt_words, xt_scales, w_words, w_scales, lo, wb_words, wb_scales, so, offs, offs2, offs3, out):
    nc = tc.nc

    def live_rows(plane, q):
        return plane[QUAD * q : QUAD * q + LIVE, :]

    def half_of(offsets, u):
        return offsets[:, HALF_COLS * u : HALF_COLS * (u + 1)]

    with ExitStack() as ctx:
        lists = ctx.enter_context(tc.tile_pool(name="lists", bufs=1))
        sb = ctx.enter_context(tc.tile_pool(name="sb", bufs=1))
        psum = ctx.enter_context(tc.psum_pool(name="psum", bufs=1))

        idx = lists.tile([P, J // GROUP], U16, name="idx")
        idx2 = lists.tile([P, O // GROUP], U16, name="idx2")
        idx3 = lists.tile([P, O // GROUP], U16, name="idx3")

        x_words = sb.tile([P, T], I32, name="x_words", align_bytes=MX_ALIGN)
        x_plane = sb.tile([P, T // WORD], I32, name="x_plane", align_bytes=MX_ALIGN)
        w_raw = sb.tile([P, 2 * R // WORD], I32, name="w_raw", align_bytes=MX_ALIGN)
        ws_rows = sb.tile([LIVE, QUADS, R // WORD], I32, name="ws_rows", align_bytes=MX_ALIGN)
        ws_plane = sb.tile([P, R // WORD], I32, name="ws_plane", align_bytes=MX_ALIGN)
        wb_plane = sb.tile([P, N // WORD], I32, name="wb_plane", align_bytes=MX_ALIGN)
        lo_sb = sb.tile([P, PACK], F32, name="lo_sb")
        so_sb = sb.tile([P, PAGES], F32, name="so_sb")
        pages = [sb.tile([P, E], F32, name="page%d" % h) for h in range(PAGES)]

        nc.vector.memset(x_plane[:], 0)
        nc.vector.memset(ws_plane[:], 0)
        for page in pages:
            nc.vector.memset(page[:], 0.0)
        nc.vector.memset(wb_plane[:], 0)

        nc.sync.dma_start(idx[:], offs)
        nc.scalar.dma_start(ws_rows[:], w_scales[0].bitcast(I32).rearrange("(q i) c -> i q c", i=LIVE))
        nc.sync.dma_start(x_words[:], xt_words[0].rearrange("p c b -> p (c b)").bitcast(I32))
        xs_rows = xt_scales[0].bitcast(I32)
        for q in range(QUADS):
            queue = nc.sync if q < QUADS // 2 else nc.scalar
            queue.dma_start(live_rows(x_plane, q), xs_rows[LIVE * q : LIVE * (q + 1), :])
        nc.sync.dma_start(w_raw[:], w_words[0].bitcast(I32))
        nc.sync.dma_start(lo_sb[:], lo.rearrange("(p t) o -> p (t o)", t=PACK))
        nc.sync.dma_start(idx2[:], offs2)

        for q in range(QUADS):
            nc.vector.tensor_copy(live_rows(ws_plane, q), ws_rows[:, q, :])
        ws_by_set = ws_plane[:].bitcast(U8).rearrange("p (m t) -> p t m", t=PACK)
        ws_dealt = [sb.tile([P, P], U8, name="ws_dealt%d" % t, align_bytes=MX_ALIGN) for t in range(PACK)]
        nc.vector.tensor_copy(ws_dealt[0][:], ws_by_set[:, 0, :])
        w_dealt = []
        for t in range(PACK):
            dealt = sb.tile([P, 2 * P], U8, name="w_dealt%d" % t, align_bytes=MX_ALIGN)
            nc.scalar.copy(dealt[:].bitcast(U16), w_raw[:].bitcast(U16)[:, t:R:PACK])
            w_dealt.append(dealt)

        xg_plane = sb.tile([P, J], U8, name="xg_plane", align_bytes=MX_ALIGN)
        xg_words = sb.tile([P, J], U32, name="xg_words", align_bytes=MX_ALIGN)
        nc.vector.tensor_copy(xg_words[:], x_words[:].bitcast(U32).indirect(idx[:]))
        nc.vector.tensor_copy(xg_plane[:], x_plane[:].bitcast(U8).indirect(idx[:]))
        for t in range(1, PACK):
            nc.vector.tensor_copy(ws_dealt[t][:], ws_by_set[:, t, :])

        wb_sb = sb.tile([P, N], I32, name="wb_sb", align_bytes=MX_ALIGN)
        wbs_rows = wb_scales[0].bitcast(I32)
        for q in range(QUADS):
            nc.sync.dma_start(live_rows(wb_plane, q), wbs_rows[LIVE * q : LIVE * (q + 1), :])
        nc.sync.dma_start(wb_sb[:], wb_words[0].rearrange("p c b -> p (c b)").bitcast(I32))
        with nc.allow_non_contiguous_dma(reason="so_sb[p, h] = so[128 h + p]: single values"):
            nc.sync.dma_start(so_sb[:], so.rearrange("(h p) o -> p (h o)", p=P))
        nc.sync.dma_start(idx3[:], offs3)

        hid = [sb.tile([P, PACK * HALF], BF16, name="hid%d" % u, align_bytes=MX_ALIGN) for u in range(HALVES)]
        a_sb = [sb.tile([P, J], F32, name="a_sb%d" % t) for t in range(PACK)]
        nb = [sb.tile([P, 1], F32, name="nb%d" % t) for t in range(PACK)]

        def fetch(t, u):
            nc.scalar.activation(
                hid[u][:, t : PACK * HALF : PACK], a_sb[t][:].indirect(half_of(idx2, u)), ACT.Exp, bias=nb[t][:]
            )

        for t in range(PACK):
            a_ps = psum.tile([P, J], F32, name="a_ps%d" % t)
            nc.tensor.matmul_mx(
                a_ps[:],
                lhsT=w_dealt[t][:].bitcast(FP4X4),
                lhsT_scale=ws_dealt[t][:],
                rhs=xg_words[:].bitcast(FP8X4),
                rhs_scale=xg_plane[:],
                start=True,
                stop=True,
            )
            top = sb.tile([P, 1], F32, name="top%d" % t)
            nc.vector.tensor_scalar(a_sb[t][:], a_ps[:], 1.0, None, ALU.mult, ALU.max, accum_out=top[:])
            nc.scalar.activation(nb[t][:], top[:], ACT.Identity, bias=lo_sb[:, t : t + 1], scale=-1.0)
            fetch(t, 0)
        for t in range(PACK):
            fetch(t, 1)

        for u in range(HALVES):
            hid_codes = sb.tile([P, HALF], U32, name="hid_codes%d" % u, align_bytes=MX_ALIGN)
            hid_plane = sb.tile([P, HALF], U8, name="hid_plane%d" % u, align_bytes=MX_ALIGN)
            nc.vector.quantize_mx(hid_codes[:].bitcast(FP8X4), hid_plane[:], hid[u][:])
            for h in range(PAGES):
                p_ps = psum.tile([P, HALF], F32, name="p_ps%d%d" % (u, h))
                nc.tensor.matmul_mx(
                    p_ps[:],
                    lhsT=wb_sb[:, h * P : (h + 1) * P].bitcast(FP8X4),
                    lhsT_scale=wb_plane[:].bitcast(U8)[:, h * P : (h + 1) * P],
                    rhs=hid_codes[:].bitcast(FP8X4),
                    rhs_scale=hid_plane[:],
                    start=True,
                    stop=True,
                )
                p_sb = sb.tile([P, HALF], F32, name="p_sb%d%d" % (u, h))
                nc.vector.tensor_copy(p_sb[:], p_ps[:])
                nc.scalar.activation(
                    pages[h][:].indirect(half_of(idx3, u)), p_sb[:], ACT.Copy, scale=so_sb[:, h : h + 1]
                )
        for h in range(PAGES):
            nc.sync.dma_start(out[h * P : (h + 1) * P, :], pages[h][:])
